import numpy as np
import ml_dtypes


def mxq(x, axis, fmt="e4m3"):
    dtype, down = {"e4m3": (ml_dtypes.float8_e4m3fn, 7), "e5m2": (ml_dtypes.float8_e5m2, 14)}[fmt]
    v = np.moveaxis(np.asarray(x, np.float32).astype(ml_dtypes.bfloat16).astype(np.float64), axis, -1)
    blocks = v.reshape(v.shape[:-1] + (-1, 32))
    amax = np.abs(blocks).max(-1, keepdims=True)
    byte = np.maximum(np.where(amax > 0, np.frexp(amax)[1] - 1 + 127, 0) - down, 1)
    scale = np.exp2(byte - 127.0)
    codes = (blocks / scale).astype(np.float32).astype(dtype).astype(np.float64)
    return np.moveaxis((codes * scale).reshape(v.shape), -1, axis)


WIDE = False


def mx_kscale(k):
    if not WIDE:
        return np.ones(k)
    levels = np.array([10, -10, 5, -5, 0])
    if k % 512:
        return np.exp2(np.random.permutation(np.resize(levels, k // 32))).repeat(32)
    a = np.empty((k // 512, 16))
    for p in range(k // 512):
        a[p, :8] = np.random.permutation(np.resize(levels, 8))
        for g in range(8):
            far = levels[np.abs(levels - a[p, g]) >= 10]
            a[p, g + 8] = far[np.random.randint(len(far))]
    return np.exp2(a.ravel()).repeat(32)


def f64(x):
    return np.asarray(x).astype(np.float64)


def striped(idx):
    return np.tile(idx.reshape(-1, 16).T, (8, 1)).astype(np.uint16)


def unstriped(offs):
    return offs[:16].T.reshape(-1).astype(np.int64)


def striped8(idx):
    return np.concatenate([x.reshape(-1, 16).T for x in idx]).astype(np.uint16)


def runs(offs, k):
    lists = np.stack([offs[16 * r : 16 * r + 16].T.reshape(-1) for r in range(8)]).astype(np.int64)
    return lists[np.arange(k) % 512 // 64]


def pack_weight(w):
    k, n = w.shape
    w = f64(np.asarray(w, np.float32).astype(ml_dtypes.bfloat16)).reshape(k // 32, 32, n)
    amax = np.abs(w).max(1)
    byte = np.clip(np.where(amax > 0, np.frexp(amax)[1] - 1 + 127 - 7, 1), 1, 254)
    scaled = (w * np.exp2(127.0 - byte)[:, None, :]).reshape(k, n).astype(np.float32)
    words = np.ascontiguousarray(scaled.reshape(k // 512, 128, 4, n).transpose(0, 1, 3, 2)).astype(ml_dtypes.float8_e4m3fn).view(np.uint8)
    return words, np.ascontiguousarray(byte.astype(np.uint8).reshape(k // 512, 16, n))


def unpack_weight(words, scales):
    g, p, n, _ = words.shape
    vals = np.ascontiguousarray(words).view(ml_dtypes.float8_e4m3fn).astype(np.float64) * np.repeat(np.exp2(scales.astype(np.float64) - 127.0), 8, axis=1)[..., None]
    return vals.transpose(0, 1, 3, 2).reshape(g * 512, n)


def sigmoid(v):
    return 1.0 / (1.0 + np.exp(-np.maximum(v, -700.0)))


K, T, S, H, W, G = 512, 1024, 256, 512, 128, 2048


def setup_inputs():
    n = np.random.standard_normal
    s = mx_kscale(K)[:, None]
    packed_xT = pack_weight(n((K, T)) * s)
    packed_dT = pack_weight(n((K, G)) / s)
    perm = np.random.permutation(S)
    return {
        "x_words": packed_xT[0],
        "x_scales": packed_xT[1],
        "w1": (n((K, H)) / np.sqrt(K) / s).astype(np.float32),
        "gs": (np.random.uniform(0.5, 1.5, (K, 1)) * s).astype(np.float32),
        "d_words": packed_dT[0],
        "d_scales": packed_dT[1],
        "sl": np.random.uniform(1.0, 2.0, (H, 1)).astype(np.float32),
        "th": (0.5 * n((H, 1))).astype(np.float32),
        "offs": striped(np.random.permutation(T)[:S]),
        "n1": striped(perm[:W]),
        "n2": striped(perm[W:]),
        "n3": striped(np.random.permutation(S)),
        "k1": striped8(np.random.randint(0, G, (8, H))),
        "k2": striped8(np.random.randint(0, G, (8, H))),
        "hz": striped8(np.random.randint(0, T, (8, S))),
        "n4": striped8(np.stack([np.random.permutation(S) for _ in range(8)])),
        "n5": striped8(np.stack([np.random.permutation(S) for _ in range(8)])),
    }


def reference(x_words, x_scales, w1, gs, d_words, d_scales, sl, th, offs, n1, n2, n3, k1, k2, hz, n4, n5):
    d_k1 = unpack_weight(d_words, d_scales)[np.arange(K)[:, None], runs(k1, K)]
    xq = unpack_weight(x_words, x_scales)[:, unstriped(offs)]
    y = mxq(f64(w1), 0, "e4m3").T @ xq
    pa = y[:, unstriped(n1)]
    pb = y[:, unstriped(n2)]
    rb = pa - pb
    ra = pa + pb
    ds = np.zeros((H, S))
    ds[:, unstriped(n1)] = ra
    dt = ds.copy()
    dt[:, unstriped(n2)] = rb
    z = f64(gs) * (np.maximum(dt, dt[:, unstriped(n3)]))
    d_k2 = unpack_weight(d_words, d_scales)[np.arange(K)[:, None], runs(k2, K)]
    x_hz = unpack_weight(x_words, x_scales)[np.arange(K)[:, None], runs(hz, K)]
    h = 0.0625 * ((d_k1.T @ mxq(z, 0, "e4m3") + d_k2.T @ x_hz))
    st = np.maximum(h, h[np.arange(H)[:, None], runs(n4, H)])
    sg = sigmoid(f64(sl) * (st[np.arange(H)[:, None], runs(n5, H)] - f64(th)))
    return st * sg

@@ -1,0 +1,243 @@
+from contextlib import ExitStack
+
+import concourse.mybir as mybir
+
+K, T, S, H, W, G = 512, 1024, 256, 512, 128, 2048
+FLOPS = 3 * 2 * K * H * S
+
+F32 = mybir.dt.float32
+BF16 = mybir.dt.bfloat16
+I32 = mybir.dt.int32
+U32 = mybir.dt.uint32
+U16 = mybir.dt.uint16
+U8 = mybir.dt.uint8
+FP8X4 = mybir.dt.float8_e4m3fn_x4
+ACT = mybir.ActivationFunctionType
+ALU = mybir.AluOpType
+
+P = 128
+PACK = 4
+HALF = S // 2
+SCALAR_M = 24
+
+
+def tile_picked_cmixhhaarhehh_none_p_kernel(
+    tc, x_words, x_scales, w1, gs, d_words, d_scales, sl, th, offs, n1, n2, n3, k1, k2, hz, n4, n5, out
+):
+    nc = tc.nc
+    planes = range(PACK)
+    halves = range(2)
+
+    with ExitStack() as ctx:
+        lists = ctx.enter_context(tc.tile_pool(name="lists", bufs=1))
+        sb = ctx.enter_context(tc.tile_pool(name="sb", bufs=1))
+        psum = ctx.enter_context(tc.psum_pool(name="psum", bufs=1))
+
+        def tile(name, shape, dtype, tag=""):
+            return sb.tile(shape, dtype, name=name, tag=tag or name, align_bytes=64)
+
+        def load_list(name, src):
+            dst = lists.tile(list(src.shape), U16, name=name)
+            nc.sync.dma_start(dst[:], src)
+            return dst
+
+        def as_words(packed):
+            return packed[0].rearrange("p n r -> p (n r)").bitcast(I32)
+
+        xs_tab = tile("xs_tab", [P, T], U8)
+        nc.vector.memset(xs_tab[:].bitcast(I32), 0)
+        ds_tab = tile("ds_tab", [P, G], U8)
+        nc.vector.memset(ds_tab[:].bitcast(I32), 0)
+        placed = tile("placed", [P, 2 * H + S], U8)
+        nc.vector.memset(placed[:].bitcast(I32), 0)
+
+        offs_l = load_list("offs_l", offs)
+        hz_l = load_list("hz_l", hz)
+        xw_tab = tile("xw_tab", [P, T], U32)
+        nc.sync.dma_start(xw_tab[:].bitcast(I32), as_words(x_words))
+        xs_rows = x_scales[0].bitcast(I32)
+        for b in range(2):
+            nc.sync.dma_start(xs_tab[b:P:16, :].bitcast(I32), xs_rows[b:16:2, :])
+        for a in (2, 3):
+            nc.sync.dma_start(xs_tab[a:P:32, :].bitcast(I32), xs_rows[a:16:4, :])
+        w_rows = w1.rearrange("(p j) c -> p j c", j=PACK)
+        w_raw = []
+        for u in halves:
+            raw = tile(f"w_raw{u}", [P, PACK, H // 2], F32)
+            nc.sync.dma_start(raw[:], w_rows[:, :, u * (H // 2) : (u + 1) * (H // 2)])
+            w_raw.append(raw)
+        n1_l = load_list("n1_l", n1)
+        n2_l = load_list("n2_l", n2)
+        k1_l = load_list("k1_l", k1)
+        k2_l = load_list("k2_l", k2)
+        dw_tab = tile("dw_tab", [P, G], U32)
+        nc.sync.dma_start(dw_tab[:].bitcast(I32), as_words(d_words))
+
+        def load_by_row(name, src):
+            dst = tile(name, [P, PACK], F32)
+            nc.sync.dma_start(dst[:], src.rearrange("(p t) o -> p (t o)", t=PACK))
+            return dst
+
+        gs_t = load_by_row("gs_t", gs)
+        n3_l = load_list("n3_l", n3)
+        n4_l = load_list("n4_l", n4)
+        n5_l = load_list("n5_l", n5)
+        sl_t = load_by_row("sl_t", sl)
+        th_t = load_by_row("th_t", th)
+
+        ds_rows = d_scales[0].bitcast(I32)
+        for b in range(2):
+            nc.gpsimd.dma_start(ds_tab[b:P:16, :].bitcast(I32), ds_rows[b:16:2, :])
+
+        xq_b = tile("xq_b", [P, S], U8)
+        xq_w = tile("xq_w", [P, S], U32)
+        nc.vector.tensor_copy(xq_b[:], xs_tab[:].indirect(offs_l[:]))
+        nc.vector.tensor_copy(xq_w[:], xw_tab[:].indirect(offs_l[:]))
+
+        hz_b = tile("hz_b", [P, S], U8)
+        hz_w = tile("hz_w", [P, S], U32)
+        nc.vector.tensor_copy(hz_b[:], xs_tab[:].indirect(hz_l[:]))
+        nc.vector.tensor_copy(hz_w[:], xw_tab[:].indirect(hz_l[:]))
+
+        w_bf = tile("w_bf", [P, PACK, P, PACK], BF16)
+
+        def deal_w(copy, u, m0, m1):
+            copy(
+                w_bf[:, :, 64 * u + m0 : 64 * u + m1, :].rearrange("p t m j -> p m j t"),
+                w_raw[u][:, :, PACK * m0 : PACK * m1].rearrange("p j (m t) -> p m j t", t=PACK),
+            )
+
+        deal_w(nc.scalar.copy, 0, 0, 64)
+        deal_w(nc.scalar.copy, 1, 0, SCALAR_M)
+        deal_w(nc.vector.tensor_copy, 1, SCALAR_M, 64)
+
+        y_ps = []
+        for t in planes:
+            w_w = tile(f"w_w{t}", [P, P], U32)
+            w_b = tile(f"w_b{t}", [P, P], U8)
+            nc.vector.quantize_mx(
+                out=w_w[:].bitcast(FP8X4), scales=w_b[:], in_=w_bf[:, t, :, :].rearrange("p m j -> p (m j)")
+            )
+            acc = psum.tile([P, S], F32, name=f"y_ps{t}", tag=f"low{t}")
+            nc.tensor.matmul_mx(
+                out=acc[:], lhsT=w_w[:].bitcast(FP8X4), lhsT_scale=w_b[:],
+                rhs=xq_w[:].bitcast(FP8X4), rhs_scale=xq_b[:], start=True, stop=True,
+            )
+            y_ps.append(acc)
+
+        y = [tile(f"y{t}", [P, S], F32) for t in planes]
+        h_win = [tile(f"h_win{t}", [P, 2 * S], F32) for t in planes]
+        st_win = [tile(f"st_win{t}", [P, 2 * S], F32) for t in planes]
+        dt = [tile(f"dt{t}", [P, S], F32) for t in planes]
+        pa = [h_win[t][:, S : S + W] for t in planes]
+        pb = [h_win[t][:, S + W :] for t in planes]
+        ra = [st_win[t][:, S : S + W] for t in planes]
+        rb = [st_win[t][:, S + W :] for t in planes]
+
+        for t in planes:
+            if t == 0:
+                nc.scalar.activation(y[t][:], y_ps[t][:], ACT.Copy)
+            else:
+                nc.vector.tensor_copy(y[t][:], y_ps[t][:])
+        for t in planes:
+            nc.scalar.activation(pa[t], y[t][:].indirect(n1_l[:]), ACT.Copy)
+            nc.scalar.activation(pb[t], y[t][:].indirect(n2_l[:]), ACT.Copy)
+            nc.vector.tensor_tensor(ra[t], pa[t], pb[t], ALU.add)
+            nc.vector.tensor_tensor(rb[t], pa[t], pb[t], ALU.subtract)
+        for t in planes:
+            nc.scalar.activation(dt[t][:].indirect(n1_l[:]), ra[t], ACT.Copy)
+        for t in planes:
+            nc.scalar.activation(dt[t][:].indirect(n2_l[:]), rb[t], ACT.Copy)
+
+        got_b = tile("got_b", [P, 2 * H], U8, tag=f"w_w{PACK - 1}")
+        nc.vector.tensor_copy(got_b[:, 0:H], ds_tab[:].indirect(k1_l[:]))
+        nc.vector.tensor_copy(got_b[:, H : 2 * H], ds_tab[:].indirect(k2_l[:]))
+        dealt_b = tile("dealt_b", [P, 2 * H + S], U8)
+        nc.vector.tensor_copy(
+            dealt_b[:, 0 : 2 * H].rearrange("p (l t m) -> p l m t", l=2, t=PACK),
+            got_b[:].rearrange("p (l m t) -> p l m t", l=2, t=PACK),
+        )
+        nc.vector.tensor_copy(dealt_b[:, 2 * H :].bitcast(I32), hz_b[:].bitcast(I32))
+        for a in range(4):
+            src = 16 * (a // 2) + a % 2
+            nc.sync.dma_start(placed[a:P:32, :].bitcast(I32), dealt_b[src:P:32, :].bitcast(I32))
+
+        got_w = tile("got_w", [P, 2 * H], U32)
+        dealt_w = tile("dealt_w", [P, 2 * H], U32)
+        for c, k_l in ((1, k2_l), (0, k1_l)):
+            cols = slice(c * H, (c + 1) * H)
+            nc.vector.tensor_copy(got_w[:, cols], dw_tab[:].indirect(k_l[:]))
+            nc.vector.tensor_copy(
+                dealt_w[:, cols].rearrange("p (t m) -> p m t", t=PACK),
+                got_w[:, cols].rearrange("p (m t) -> p m t", t=PACK),
+            )
+
+        nbias = tile("nbias", [P, PACK], F32)
+        sl_th = tile("sl_th", [P, PACK], F32)
+        nc.gpsimd.tensor_tensor(sl_th[:], sl_t[:], th_t[:], ALU.mult)
+        nc.gpsimd.tensor_scalar(nbias[:], sl_th[:], -1.0, 0.0, ALU.mult, ALU.add)
+
+        h_ps = {}
+        for u in halves:
+            for t in planes:
+                acc = psum.tile([P, HALF], F32, name=f"h_ps{u}{t}", tag=(f"low{t}" if u else f"high{t}"))
+                cols = slice(H + t * P, H + (t + 1) * P)
+                nc.tensor.matmul_mx(
+                    out=acc[:], lhsT=dealt_w[:, cols].bitcast(FP8X4), lhsT_scale=placed[:, cols],
+                    rhs=hz_w[:, u * HALF : (u + 1) * HALF].bitcast(FP8X4),
+                    rhs_scale=placed[:, 2 * H + u * HALF : 2 * H + (u + 1) * HALF],
+                    start=True, stop=False,
+                )
+                h_ps[u, t] = acc
+
+        for u in halves:
+            js = slice(u * HALF, (u + 1) * HALF)
+            z_bf = tile(f"z_bf{u}", [P, HALF, PACK], BF16)
+            top = [tile(f"top{u}{t}", [P, HALF], F32) for t in planes]
+            for t in planes:
+                far = tile(f"far{u}{t}", [P, HALF], F32)
+                nc.scalar.activation(far[:], dt[t][:].indirect(n3_l[:, u * 8 : (u + 1) * 8]), ACT.Copy)
+                nc.vector.tensor_tensor(top[t][:], dt[t][:, js], far[:], ALU.max)
+                nc.vector.tensor_scalar(z_bf[:, :, t], top[t][:], gs_t[:, t : t + 1], None, ALU.mult)
+            z_w = tile(f"z_w{u}", [P, HALF], U32)
+            z_b = tile(f"z_b{u}", [P, HALF], U8)
+            nc.vector.quantize_mx(
+                out=z_w[:].bitcast(FP8X4), scales=z_b[:], in_=z_bf[:].rearrange("p j t -> p (j t)")
+            )
+            for t in planes:
+                cols = slice(t * P, (t + 1) * P)
+                nc.tensor.matmul_mx(
+                    out=h_ps[u, t][:], lhsT=dealt_w[:, cols].bitcast(FP8X4), lhsT_scale=placed[:, cols],
+                    rhs=z_w[:].bitcast(FP8X4), rhs_scale=z_b[:], start=False, stop=True,
+                )
+
+        for t in planes:
+            nc.scalar.activation(h_win[t][:, 0:HALF], h_ps[0, t][:], ACT.Copy, scale=0.0625)
+        for t in planes:
+            if t == 0:
+                nc.scalar.activation(h_win[t][:, HALF:S], h_ps[1, t][:], ACT.Copy, scale=0.0625)
+            else:
+                nc.vector.tensor_scalar(h_win[t][:, HALF:S], h_ps[1, t][:], 0.0625, None, ALU.mult)
+
+        out_rows = out.rearrange("(p t) j -> p t j", t=PACK)
+
+        def neighbour(t):
+            near = tile(f"near{t}", [P, S], F32)
+            nc.scalar.activation(near[:], h_win[t][:].indirect(n4_l[:]), ACT.Copy)
+            nc.vector.tensor_tensor(st_win[t][:, 0:S], h_win[t][:, 0:S], near[:], ALU.max)
+
+        def gate(t):
+            sg = tile(f"sg{t}", [P, S], F32)
+            nc.scalar.activation(
+                sg[:], st_win[t][:].indirect(n5_l[:]), ACT.Sigmoid,
+                bias=nbias[:, t : t + 1], scale=sl_t[:, t : t + 1],
+            )
+            res = tile(f"res{t}", [P, S], F32)
+            nc.vector.tensor_tensor(res[:], st_win[t][:, 0:S], sg[:], ALU.mult)
+            nc.sync.dma_start(out_rows[:, t, :], res[:])
+
+        neighbour(0)
+        for t in planes:
+            if t + 1 < PACK:
+                neighbour(t + 1)
+            gate(t)

@@ -44,6 +44,11 @@ def tile_picked_cmixhhaarhehh_none_p_kernel(
         def as_words(packed):
             return packed[0].rearrange("p n r -> p (n r)").bitcast(I32)
 
+        warm_in = tile("warm_in", [P, 1], F32)
+        warm_out = tile("warm_out", [P, 1], F32)
+        nc.gpsimd.memset(warm_in[:], 0.0)
+        nc.scalar.activation(warm_out[:], warm_in[:], ACT.Sigmoid)
+
         xs_tab = tile("xs_tab", [P, T], U8)
         nc.vector.memset(xs_tab[:].bitcast(I32), 0)
         ds_tab = tile("ds_tab", [P, G], U8)

@@ -27,6 +27,7 @@ def tile_picked_cmixhhaarhehh_none_p_kernel(
     nc = tc.nc
     planes = range(PACK)
     halves = range(2)
+    last = PACK - 1
 
     with ExitStack() as ctx:
         lists = ctx.enter_context(tc.tile_pool(name="lists", bufs=1))
@@ -44,18 +45,23 @@ def tile_picked_cmixhhaarhehh_none_p_kernel(
         def as_words(packed):
             return packed[0].rearrange("p n r -> p (n r)").bitcast(I32)
 
+        xs_tab = tile("xs_tab", [P, T], U8)
+        nc.vector.memset(xs_tab[:].bitcast(I32), 0)
+
         warm_in = tile("warm_in", [P, 1], F32)
         warm_out = tile("warm_out", [P, 1], F32)
         nc.gpsimd.memset(warm_in[:], 0.0)
         nc.scalar.activation(warm_out[:], warm_in[:], ACT.Sigmoid)
 
-        xs_tab = tile("xs_tab", [P, T], U8)
-        nc.vector.memset(xs_tab[:].bitcast(I32), 0)
         ds_tab = tile("ds_tab", [P, G], U8)
-        nc.vector.memset(ds_tab[:].bitcast(I32), 0)
-        placed = tile("placed", [P, 2 * H + S], U8)
+        nc.gpsimd.memset(ds_tab[:].bitcast(I32), 0)
+        placed = tile("placed", [P, H], U8)
         nc.vector.memset(placed[:].bitcast(I32), 0)
+        hz_s = tile("hz_s", [P, S], U8)
+        nc.vector.memset(hz_s[:].bitcast(I32), 0)
 
+        w_rows = w1.rearrange("(p j) c -> p j c", j=PACK)
+        w_raw = [tile(f"w_raw{u}", [P, PACK, H // 2], F32) for u in halves]
         offs_l = load_list("offs_l", offs)
         hz_l = load_list("hz_l", hz)
         xw_tab = tile("xw_tab", [P, T], U32)
@@ -65,16 +71,13 @@ def tile_picked_cmixhhaarhehh_none_p_kernel(
             nc.sync.dma_start(xs_tab[b:P:16, :].bitcast(I32), xs_rows[b:16:2, :])
         for a in (2, 3):
             nc.sync.dma_start(xs_tab[a:P:32, :].bitcast(I32), xs_rows[a:16:4, :])
-        w_rows = w1.rearrange("(p j) c -> p j c", j=PACK)
-        w_raw = []
-        for u in halves:
-            raw = tile(f"w_raw{u}", [P, PACK, H // 2], F32)
-            nc.sync.dma_start(raw[:], w_rows[:, :, u * (H // 2) : (u + 1) * (H // 2)])
-            w_raw.append(raw)
+        nc.sync.dma_start(w_raw[0][:], w_rows[:, :, 0 : H // 2])
+        nc.sync.dma_start(w_raw[1][:], w_rows[:, :, H // 2 : H])
         n1_l = load_list("n1_l", n1)
         n2_l = load_list("n2_l", n2)
-        k1_l = load_list("k1_l", k1)
         k2_l = load_list("k2_l", k2)
+        n3_l = load_list("n3_l", n3)
+        k1_l = load_list("k1_l", k1)
         dw_tab = tile("dw_tab", [P, G], U32)
         nc.sync.dma_start(dw_tab[:].bitcast(I32), as_words(d_words))
 
@@ -84,7 +87,6 @@ def tile_picked_cmixhhaarhehh_none_p_kernel(
             return dst
 
         gs_t = load_by_row("gs_t", gs)
-        n3_l = load_list("n3_l", n3)
         n4_l = load_list("n4_l", n4)
         n5_l = load_list("n5_l", n5)
         sl_t = load_by_row("sl_t", sl)
@@ -98,10 +100,7 @@ def tile_picked_cmixhhaarhehh_none_p_kernel(
         xq_w = tile("xq_w", [P, S], U32)
         nc.vector.tensor_copy(xq_b[:], xs_tab[:].indirect(offs_l[:]))
         nc.vector.tensor_copy(xq_w[:], xw_tab[:].indirect(offs_l[:]))
-
-        hz_b = tile("hz_b", [P, S], U8)
         hz_w = tile("hz_w", [P, S], U32)
-        nc.vector.tensor_copy(hz_b[:], xs_tab[:].indirect(hz_l[:]))
         nc.vector.tensor_copy(hz_w[:], xw_tab[:].indirect(hz_l[:]))
 
         w_bf = tile("w_bf", [P, PACK, P, PACK], BF16)
@@ -116,133 +115,161 @@ def tile_picked_cmixhhaarhehh_none_p_kernel(
         deal_w(nc.scalar.copy, 1, 0, SCALAR_M)
         deal_w(nc.vector.tensor_copy, 1, SCALAR_M, 64)
 
+        w_w = [tile(f"w_w{t}", [P, P], U32) for t in planes]
+        w_b = [tile(f"w_b{t}", [P, P], U8) for t in planes]
+        for t in planes:
+            nc.vector.quantize_mx(
+                out=w_w[t][:].bitcast(FP8X4), scales=w_b[t][:], in_=w_bf[:, t, :, :].rearrange("p m j -> p (m j)")
+            )
         y_ps = []
         for t in planes:
-            w_w = tile(f"w_w{t}", [P, P], U32)
-            w_b = tile(f"w_b{t}", [P, P], U8)
-            nc.vector.quantize_mx(
-                out=w_w[:].bitcast(FP8X4), scales=w_b[:], in_=w_bf[:, t, :, :].rearrange("p m j -> p (m j)")
-            )
-            acc = psum.tile([P, S], F32, name=f"y_ps{t}", tag=f"low{t}")
+            acc = psum.tile([P, S], F32, name=f"y_ps{t}", tag=f"h_ps{t}_0")
             nc.tensor.matmul_mx(
-                out=acc[:], lhsT=w_w[:].bitcast(FP8X4), lhsT_scale=w_b[:],
+                out=acc[:], lhsT=w_w[t][:].bitcast(FP8X4), lhsT_scale=w_b[t][:],
                 rhs=xq_w[:].bitcast(FP8X4), rhs_scale=xq_b[:], start=True, stop=True,
             )
             y_ps.append(acc)
 
-        y = [tile(f"y{t}", [P, S], F32) for t in planes]
+        dt_win = [tile(f"dt_win{t}", [P, 2 * S], F32) for t in planes]
         h_win = [tile(f"h_win{t}", [P, 2 * S], F32) for t in planes]
         st_win = [tile(f"st_win{t}", [P, 2 * S], F32) for t in planes]
-        dt = [tile(f"dt{t}", [P, S], F32) for t in planes]
-        pa = [h_win[t][:, S : S + W] for t in planes]
-        pb = [h_win[t][:, S + W :] for t in planes]
-        ra = [st_win[t][:, S : S + W] for t in planes]
-        rb = [st_win[t][:, S + W :] for t in planes]
+        y = [dt_win[t][:, S:] for t in planes]
+        far = [h_win[t][:, S:] for t in planes]
+        near = [st_win[t][:, S:] for t in planes]
+        pa, pb, ra, rb = (
+            [tile(f"{name}{u}", [P, 2 * W], F32) for u in halves] for name in ("pa", "pb", "ra", "rb")
+        )
+
+        def of(pairs, t):
+            return pairs[t // 2][:, t % 2 * W : (t % 2 + 1) * W]
 
         for t in planes:
             if t == 0:
-                nc.scalar.activation(y[t][:], y_ps[t][:], ACT.Copy)
+                nc.scalar.activation(y[t], y_ps[t][:], ACT.Copy)
             else:
-                nc.vector.tensor_copy(y[t][:], y_ps[t][:])
+                nc.vector.tensor_copy(y[t], y_ps[t][:])
         for t in planes:
-            nc.scalar.activation(pa[t], y[t][:].indirect(n1_l[:]), ACT.Copy)
-            nc.scalar.activation(pb[t], y[t][:].indirect(n2_l[:]), ACT.Copy)
-            nc.vector.tensor_tensor(ra[t], pa[t], pb[t], ALU.add)
-            nc.vector.tensor_tensor(rb[t], pa[t], pb[t], ALU.subtract)
-        for t in planes:
-            nc.scalar.activation(dt[t][:].indirect(n1_l[:]), ra[t], ACT.Copy)
-        for t in planes:
-            nc.scalar.activation(dt[t][:].indirect(n2_l[:]), rb[t], ACT.Copy)
+            nc.scalar.activation(of(pa, t), y[t].indirect(n1_l[:]), ACT.Copy)
+            nc.scalar.activation(of(pb, t), y[t].indirect(n2_l[:]), ACT.Copy)
+            if t % 2:
+                u = t // 2
+                nc.vector.tensor_tensor(ra[u][:], pa[u][:], pb[u][:], ALU.add)
+                nc.vector.tensor_tensor(rb[u][:], pa[u][:], pb[u][:], ALU.subtract)
 
-        got_b = tile("got_b", [P, 2 * H], U8, tag=f"w_w{PACK - 1}")
-        nc.vector.tensor_copy(got_b[:, 0:H], ds_tab[:].indirect(k1_l[:]))
-        nc.vector.tensor_copy(got_b[:, H : 2 * H], ds_tab[:].indirect(k2_l[:]))
-        dealt_b = tile("dealt_b", [P, 2 * H + S], U8)
-        nc.vector.tensor_copy(
-            dealt_b[:, 0 : 2 * H].rearrange("p (l t m) -> p l m t", l=2, t=PACK),
-            got_b[:].rearrange("p (l m t) -> p l m t", l=2, t=PACK),
-        )
-        nc.vector.tensor_copy(dealt_b[:, 2 * H :].bitcast(I32), hz_b[:].bitcast(I32))
-        for a in range(4):
-            src = 16 * (a // 2) + a % 2
-            nc.sync.dma_start(placed[a:P:32, :].bitcast(I32), dealt_b[src:P:32, :].bitcast(I32))
+        hz_b = tile("hz_b", [P, S], U8, tag=f"w_w{last}")
+        nc.vector.tensor_copy(hz_b[:], xs_tab[:].indirect(hz_l[:]))
+        k2_b = tile("k2_b", [P, H], U8, tag="pa0")
+        k1_b = tile("k1_b", [P, H], U8, tag="pa1")
+        nc.vector.tensor_copy(k2_b[:], ds_tab[:].indirect(k2_l[:]))
+        nc.vector.tensor_copy(k1_b[:], ds_tab[:].indirect(k1_l[:]))
+        for dst, first, got in ((hz_s, 0, hz_b), (placed, 4, k2_b), (placed, 0, k1_b)):
+            for a in range(4):
+                src = 16 * (a // 2) + a % 2
+                nc.sync.dma_start(dst[first + a : P : 32, :].bitcast(I32), got[src:P:32, :].bitcast(I32))
 
         got_w = tile("got_w", [P, 2 * H], U32)
         dealt_w = tile("dealt_w", [P, 2 * H], U32)
         for c, k_l in ((1, k2_l), (0, k1_l)):
+            nc.vector.tensor_copy(got_w[:, c * H : (c + 1) * H], dw_tab[:].indirect(k_l[:]))
+        for c in (1, 0):
             cols = slice(c * H, (c + 1) * H)
-            nc.vector.tensor_copy(got_w[:, cols], dw_tab[:].indirect(k_l[:]))
             nc.vector.tensor_copy(
-                dealt_w[:, cols].rearrange("p (t m) -> p m t", t=PACK),
-                got_w[:, cols].rearrange("p (m t) -> p m t", t=PACK),
+                dealt_w[:, cols].rearrange("p (t g i) -> p g t i", t=PACK, i=4),
+                got_w[:, cols].rearrange("p (g i t) -> p g t i", t=PACK, i=4),
             )
+        dealt_b = tile("dealt_b", [P, H], U8)
+        nc.vector.tensor_copy(
+            dealt_b[:].rearrange("p (t g i) -> p g t i", t=PACK, i=16),
+            placed[:].rearrange("p (g i t) -> p g t i", t=PACK, i=16),
+        )
 
-        nbias = tile("nbias", [P, PACK], F32)
-        sl_th = tile("sl_th", [P, PACK], F32)
-        nc.gpsimd.tensor_tensor(sl_th[:], sl_t[:], th_t[:], ALU.mult)
-        nc.gpsimd.tensor_scalar(nbias[:], sl_th[:], -1.0, 0.0, ALU.mult, ALU.add)
+        nbias = tile("nbias", [P, PACK], F32, tag="pb1")
+        nc.vector.scalar_tensor_tensor(nbias[:], sl_t[:], -1.0, th_t[:], ALU.mult, ALU.mult)
 
+        parts = [(0, 0, HALF), (0, HALF, S)] + [(t, 0, S) for t in range(1, PACK)]
         h_ps = {}
-        for u in halves:
-            for t in planes:
-                acc = psum.tile([P, HALF], F32, name=f"h_ps{u}{t}", tag=(f"low{t}" if u else f"high{t}"))
-                cols = slice(H + t * P, H + (t + 1) * P)
-                nc.tensor.matmul_mx(
-                    out=acc[:], lhsT=dealt_w[:, cols].bitcast(FP8X4), lhsT_scale=placed[:, cols],
-                    rhs=hz_w[:, u * HALF : (u + 1) * HALF].bitcast(FP8X4),
-                    rhs_scale=placed[:, 2 * H + u * HALF : 2 * H + (u + 1) * HALF],
-                    start=True, stop=False,
-                )
-                h_ps[u, t] = acc
-
-        for u in halves:
-            js = slice(u * HALF, (u + 1) * HALF)
-            z_bf = tile(f"z_bf{u}", [P, HALF, PACK], BF16)
-            top = [tile(f"top{u}{t}", [P, HALF], F32) for t in planes]
-            for t in planes:
-                far = tile(f"far{u}{t}", [P, HALF], F32)
-                nc.scalar.activation(far[:], dt[t][:].indirect(n3_l[:, u * 8 : (u + 1) * 8]), ACT.Copy)
-                nc.vector.tensor_tensor(top[t][:], dt[t][:, js], far[:], ALU.max)
-                nc.vector.tensor_scalar(z_bf[:, :, t], top[t][:], gs_t[:, t : t + 1], None, ALU.mult)
-            z_w = tile(f"z_w{u}", [P, HALF], U32)
-            z_b = tile(f"z_b{u}", [P, HALF], U8)
-            nc.vector.quantize_mx(
-                out=z_w[:].bitcast(FP8X4), scales=z_b[:], in_=z_bf[:].rearrange("p j t -> p (j t)")
+        for t, j0, j1 in parts:
+            acc = psum.tile([P, j1 - j0], F32, name=f"h_ps{t}_{j0}")
+            cols = slice(H + t * P, H + (t + 1) * P)
+            nc.tensor.matmul_mx(
+                out=acc[:], lhsT=dealt_w[:, cols].bitcast(FP8X4), lhsT_scale=dealt_b[4:P, t * P : (t + 1) * P],
+                rhs=hz_w[:, j0:j1].bitcast(FP8X4), rhs_scale=hz_s[:, j0:j1],
+                start=True, stop=False,
             )
-            for t in planes:
-                cols = slice(t * P, (t + 1) * P)
-                nc.tensor.matmul_mx(
-                    out=h_ps[u, t][:], lhsT=dealt_w[:, cols].bitcast(FP8X4), lhsT_scale=placed[:, cols],
-                    rhs=z_w[:].bitcast(FP8X4), rhs_scale=z_b[:], start=False, stop=True,
-                )
+            h_ps[t, j0] = acc
 
-        for t in planes:
-            nc.scalar.activation(h_win[t][:, 0:HALF], h_ps[0, t][:], ACT.Copy, scale=0.0625)
-        for t in planes:
+        z_bf = tile("z_bf", [P, S, PACK], BF16, tag="got_w")
+        top = tile("top", [P, PACK * S], F32, tag="placed")
+
+        def put_sum(t):
+            nc.scalar.activation(dt_win[t][:].indirect(n1_l[:]), of(ra, t), ACT.Copy)
+
+        def put_difference(t):
+            nc.scalar.activation(dt_win[t][:].indirect(n2_l[:]), of(rb, t), ACT.Copy)
+
+        def make_z(t, j0, j1):
+            nc.scalar.activation(far[t][:, j0:j1], dt_win[t][:].indirect(n3_l[:, j0 // 16 : j1 // 16]), ACT.Copy)
+            larger = top[:, t * S + j0 : t * S + j1]
+            nc.vector.tensor_tensor(larger, dt_win[t][:, j0:j1], far[t][:, j0:j1], ALU.max)
+            nc.vector.tensor_scalar(z_bf[:, j0:j1, t], larger, gs_t[:, t : t + 1], None, ALU.mult)
+
+        z_w = tile("z_w", [P, S], U32)
+        z_b = tile("z_b", [P, S], U8)
+
+        def quantise_z(j0, j1):
+            nc.vector.quantize_mx(
+                out=z_w[:, j0:j1].bitcast(FP8X4), scales=z_b[:, j0:j1],
+                in_=z_bf[:, j0:j1, :].rearrange("p j t -> p (j t)"),
+            )
+
+        put_sum(0)
+        put_sum(1)
+        put_difference(0)
+        put_sum(2)
+        put_difference(1)
+        make_z(0, 0, S)
+        put_difference(2)
+        make_z(1, 0, S)
+        put_sum(3)
+        make_z(2, 0, HALF)
+        put_difference(3)
+        make_z(2, HALF, S)
+        make_z(3, 0, HALF)
+        quantise_z(0, HALF)
+        make_z(3, HALF, S)
+        quantise_z(HALF, S)
+
+        for t, j0, j1 in parts:
+            cols = slice(t * P, (t + 1) * P)
+            acc = h_ps[t, j0]
+            nc.tensor.matmul_mx(
+                out=acc[:], lhsT=dealt_w[:, cols].bitcast(FP8X4), lhsT_scale=dealt_b[:, cols],
+                rhs=z_w[:, j0:j1].bitcast(FP8X4), rhs_scale=z_b[:, j0:j1], start=False, stop=True,
+            )
             if t == 0:
-                nc.scalar.activation(h_win[t][:, HALF:S], h_ps[1, t][:], ACT.Copy, scale=0.0625)
+                nc.scalar.activation(h_win[t][:, j0:j1], acc[:], ACT.Copy, scale=0.0625)
             else:
-                nc.vector.tensor_scalar(h_win[t][:, HALF:S], h_ps[1, t][:], 0.0625, None, ALU.mult)
+                nc.vector.tensor_scalar(h_win[t][:, j0:j1], acc[:], 0.0625, None, ALU.mult)
 
         out_rows = out.rearrange("(p t) j -> p t j", t=PACK)
 
         def neighbour(t):
-            near = tile(f"near{t}", [P, S], F32)
-            nc.scalar.activation(near[:], h_win[t][:].indirect(n4_l[:]), ACT.Copy)
-            nc.vector.tensor_tensor(st_win[t][:, 0:S], h_win[t][:, 0:S], near[:], ALU.max)
+            nc.scalar.activation(near[t], h_win[t][:].indirect(n4_l[:]), ACT.Copy)
+            nc.vector.tensor_tensor(st_win[t][:, 0:S], h_win[t][:, 0:S], near[t], ALU.max)
 
-        def gate(t):
-            sg = tile(f"sg{t}", [P, S], F32)
+        def gate(t, j0, j1):
+            sg = tile(f"sg{t}_{j0}", [P, j1 - j0], F32)
             nc.scalar.activation(
-                sg[:], st_win[t][:].indirect(n5_l[:]), ACT.Sigmoid,
+                sg[:], st_win[t][:].indirect(n5_l[:, j0 // 16 : j1 // 16]), ACT.Sigmoid,
                 bias=nbias[:, t : t + 1], scale=sl_t[:, t : t + 1],
             )
-            res = tile(f"res{t}", [P, S], F32)
-            nc.vector.tensor_tensor(res[:], st_win[t][:, 0:S], sg[:], ALU.mult)
-            nc.sync.dma_start(out_rows[:, t, :], res[:])
+            res = tile(f"res{t}_{j0}", [P, j1 - j0], F32)
+            nc.vector.tensor_tensor(res[:], st_win[t][:, j0:j1], sg[:], ALU.mult)
+            nc.sync.dma_start(out_rows[:, t, j0:j1], res[:])
 
         neighbour(0)
-        for t in planes:
-            if t + 1 < PACK:
-                neighbour(t + 1)
-            gate(t)
+        for t in range(last):
+            neighbour(t + 1)
+            gate(t, 0, S)
+        gate(last, 0, HALF)
+        gate(last, HALF, S)

@@ -18,7 +18,7 @@ ALU = mybir.AluOpType
 P = 128
 PACK = 4
 HALF = S // 2
-SCALAR_M = 24
+SCALAR_M = 18
 
 
 def tile_picked_cmixhhaarhehh_none_p_kernel(
@@ -54,14 +54,12 @@ def tile_picked_cmixhhaarhehh_none_p_kernel(
         nc.scalar.activation(warm_out[:], warm_in[:], ACT.Sigmoid)
 
         ds_tab = tile("ds_tab", [P, G], U8)
-        nc.gpsimd.memset(ds_tab[:].bitcast(I32), 0)
+        nc.vector.memset(ds_tab[:].bitcast(I32), 0)
         placed = tile("placed", [P, H], U8)
         nc.vector.memset(placed[:].bitcast(I32), 0)
         hz_s = tile("hz_s", [P, S], U8)
         nc.vector.memset(hz_s[:].bitcast(I32), 0)
 
-        w_rows = w1.rearrange("(p j) c -> p j c", j=PACK)
-        w_raw = [tile(f"w_raw{u}", [P, PACK, H // 2], F32) for u in halves]
         offs_l = load_list("offs_l", offs)
         hz_l = load_list("hz_l", hz)
         xw_tab = tile("xw_tab", [P, T], U32)
@@ -71,11 +69,16 @@ def tile_picked_cmixhhaarhehh_none_p_kernel(
             nc.sync.dma_start(xs_tab[b:P:16, :].bitcast(I32), xs_rows[b:16:2, :])
         for a in (2, 3):
             nc.sync.dma_start(xs_tab[a:P:32, :].bitcast(I32), xs_rows[a:16:4, :])
-        nc.sync.dma_start(w_raw[0][:], w_rows[:, :, 0 : H // 2])
-        nc.sync.dma_start(w_raw[1][:], w_rows[:, :, H // 2 : H])
+        w_rows = w1.rearrange("(p j) c -> p j c", j=PACK)
+        w_raw = [tile(f"w_raw{u}", [P, PACK, H // 2], F32) for u in halves]
+        for u in halves:
+            nc.sync.dma_start(w_raw[u][:], w_rows[:, :, u * (H // 2) : (u + 1) * (H // 2)])
+        ds_rows = d_scales[0].bitcast(I32)
+        for b in range(2):
+            nc.sync.dma_start(ds_tab[b:P:16, :].bitcast(I32), ds_rows[b:16:2, :])
+        k2_l = load_list("k2_l", k2)
         n1_l = load_list("n1_l", n1)
         n2_l = load_list("n2_l", n2)
-        k2_l = load_list("k2_l", k2)
         n3_l = load_list("n3_l", n3)
         k1_l = load_list("k1_l", k1)
         dw_tab = tile("dw_tab", [P, G], U32)
@@ -92,10 +95,6 @@ def tile_picked_cmixhhaarhehh_none_p_kernel(
         sl_t = load_by_row("sl_t", sl)
         th_t = load_by_row("th_t", th)
 
-        ds_rows = d_scales[0].bitcast(I32)
-        for b in range(2):
-            nc.gpsimd.dma_start(ds_tab[b:P:16, :].bitcast(I32), ds_rows[b:16:2, :])
-
         xq_b = tile("xq_b", [P, S], U8)
         xq_w = tile("xq_w", [P, S], U32)
         nc.vector.tensor_copy(xq_b[:], xs_tab[:].indirect(offs_l[:]))
@@ -107,8 +106,8 @@ def tile_picked_cmixhhaarhehh_none_p_kernel(
 
         def deal_w(copy, u, m0, m1):
             copy(
-                w_bf[:, :, 64 * u + m0 : 64 * u + m1, :].rearrange("p t m j -> p m j t"),
-                w_raw[u][:, :, PACK * m0 : PACK * m1].rearrange("p j (m t) -> p m j t", t=PACK),
+                w_bf[:, :, 64 * u + m0 : 64 * u + m1, :].rearrange("p t m j -> p m t j"),
+                w_raw[u][:, :, PACK * m0 : PACK * m1].rearrange("p j (m t) -> p m t j", t=PACK),
             )
 
         deal_w(nc.scalar.copy, 0, 0, 64)
@@ -121,14 +120,15 @@ def tile_picked_cmixhhaarhehh_none_p_kernel(
             nc.vector.quantize_mx(
                 out=w_w[t][:].bitcast(FP8X4), scales=w_b[t][:], in_=w_bf[:, t, :, :].rearrange("p m j -> p (m j)")
             )
-        y_ps = []
-        for t in planes:
-            acc = psum.tile([P, S], F32, name=f"y_ps{t}", tag=f"h_ps{t}_0")
+        parts = [(0, 0, HALF), (0, HALF, S)] + [(t, 0, S) for t in range(1, PACK)]
+        y_ps = {}
+        for t, j0, j1 in parts:
+            acc = psum.tile([P, j1 - j0], F32, name=f"y_ps{t}_{j0}", tag=f"bank{t}_{j0}")
             nc.tensor.matmul_mx(
                 out=acc[:], lhsT=w_w[t][:].bitcast(FP8X4), lhsT_scale=w_b[t][:],
-                rhs=xq_w[:].bitcast(FP8X4), rhs_scale=xq_b[:], start=True, stop=True,
+                rhs=xq_w[:, j0:j1].bitcast(FP8X4), rhs_scale=xq_b[:, j0:j1], start=True, stop=True,
             )
-            y_ps.append(acc)
+            y_ps[t, j0] = acc
 
         dt_win = [tile(f"dt_win{t}", [P, 2 * S], F32) for t in planes]
         h_win = [tile(f"h_win{t}", [P, 2 * S], F32) for t in planes]
@@ -143,11 +143,11 @@ def tile_picked_cmixhhaarhehh_none_p_kernel(
         def of(pairs, t):
             return pairs[t // 2][:, t % 2 * W : (t % 2 + 1) * W]
 
-        for t in planes:
+        for t, j0, j1 in parts:
             if t == 0:
-                nc.scalar.activation(y[t], y_ps[t][:], ACT.Copy)
+                nc.scalar.activation(y[t][:, j0:j1], y_ps[t, j0][:], ACT.Copy)
             else:
-                nc.vector.tensor_copy(y[t], y_ps[t][:])
+                nc.vector.tensor_copy(y[t][:, j0:j1], y_ps[t, j0][:])
         for t in planes:
             nc.scalar.activation(of(pa, t), y[t].indirect(n1_l[:]), ACT.Copy)
             nc.scalar.activation(of(pb, t), y[t].indirect(n2_l[:]), ACT.Copy)
@@ -186,10 +186,9 @@ def tile_picked_cmixhhaarhehh_none_p_kernel(
         nbias = tile("nbias", [P, PACK], F32, tag="pb1")
         nc.vector.scalar_tensor_tensor(nbias[:], sl_t[:], -1.0, th_t[:], ALU.mult, ALU.mult)
 
-        parts = [(0, 0, HALF), (0, HALF, S)] + [(t, 0, S) for t in range(1, PACK)]
         h_ps = {}
         for t, j0, j1 in parts:
-            acc = psum.tile([P, j1 - j0], F32, name=f"h_ps{t}_{j0}")
+            acc = psum.tile([P, j1 - j0], F32, name=f"h_ps{t}_{j0}", tag=f"bank{t}_{j0}")
             cols = slice(H + t * P, H + (t + 1) * P)
             nc.tensor.matmul_mx(
                 out=acc[:], lhsT=dealt_w[:, cols].bitcast(FP8X4), lhsT_scale=dealt_b[4:P, t * P : (t + 1) * P],
@@ -236,8 +235,10 @@ def tile_picked_cmixhhaarhehh_none_p_kernel(
         make_z(2, HALF, S)
         make_z(3, 0, HALF)
         quantise_z(0, HALF)
-        make_z(3, HALF, S)
-        quantise_z(HALF, S)
+        make_z(3, HALF, S - 64)
+        quantise_z(HALF, S - 64)
+        make_z(3, S - 64, S)
+        quantise_z(S - 64, S)
 
         for t, j0, j1 in parts:
             cols = slice(t * P, (t + 1) * P)

@@ -18,7 +18,7 @@ ALU = mybir.AluOpType
 P = 128
 PACK = 4
 HALF = S // 2
-SCALAR_M = 18
+SCALAR_M = 22
 
 
 def tile_picked_cmixhhaarhehh_none_p_kernel(
@@ -60,19 +60,19 @@ def tile_picked_cmixhhaarhehh_none_p_kernel(
         hz_s = tile("hz_s", [P, S], U8)
         nc.vector.memset(hz_s[:].bitcast(I32), 0)
 
+        w_rows = w1.rearrange("(p j) c -> p j c", j=PACK)
+        w_raw = [tile(f"w_raw{u}", [P, PACK, H // 2], F32) for u in halves]
+        nc.sync.dma_start(w_raw[0][:], w_rows[:, :, 0 : H // 2])
         offs_l = load_list("offs_l", offs)
-        hz_l = load_list("hz_l", hz)
-        xw_tab = tile("xw_tab", [P, T], U32)
-        nc.sync.dma_start(xw_tab[:].bitcast(I32), as_words(x_words))
         xs_rows = x_scales[0].bitcast(I32)
         for b in range(2):
             nc.sync.dma_start(xs_tab[b:P:16, :].bitcast(I32), xs_rows[b:16:2, :])
         for a in (2, 3):
             nc.sync.dma_start(xs_tab[a:P:32, :].bitcast(I32), xs_rows[a:16:4, :])
-        w_rows = w1.rearrange("(p j) c -> p j c", j=PACK)
-        w_raw = [tile(f"w_raw{u}", [P, PACK, H // 2], F32) for u in halves]
-        for u in halves:
-            nc.sync.dma_start(w_raw[u][:], w_rows[:, :, u * (H // 2) : (u + 1) * (H // 2)])
+        nc.sync.dma_start(w_raw[1][:], w_rows[:, :, H // 2 : H])
+        xw_tab = tile("xw_tab", [P, T], U32)
+        nc.sync.dma_start(xw_tab[:].bitcast(I32), as_words(x_words))
+        hz_l = load_list("hz_l", hz)
         ds_rows = d_scales[0].bitcast(I32)
         for b in range(2):
             nc.sync.dma_start(ds_tab[b:P:16, :].bitcast(I32), ds_rows[b:16:2, :])
@@ -98,9 +98,6 @@ def tile_picked_cmixhhaarhehh_none_p_kernel(
         xq_b = tile("xq_b", [P, S], U8)
         xq_w = tile("xq_w", [P, S], U32)
         nc.vector.tensor_copy(xq_b[:], xs_tab[:].indirect(offs_l[:]))
-        nc.vector.tensor_copy(xq_w[:], xw_tab[:].indirect(offs_l[:]))
-        hz_w = tile("hz_w", [P, S], U32)
-        nc.vector.tensor_copy(hz_w[:], xw_tab[:].indirect(hz_l[:]))
 
         w_bf = tile("w_bf", [P, PACK, P, PACK], BF16)
 
@@ -120,6 +117,8 @@ def tile_picked_cmixhhaarhehh_none_p_kernel(
             nc.vector.quantize_mx(
                 out=w_w[t][:].bitcast(FP8X4), scales=w_b[t][:], in_=w_bf[:, t, :, :].rearrange("p m j -> p (m j)")
             )
+        for j0 in (0, HALF):
+            nc.vector.tensor_copy(xq_w[:, j0 : j0 + HALF], xw_tab[:].indirect(offs_l[:, j0 // 16 : (j0 + HALF) // 16]))
         parts = [(0, 0, HALF), (0, HALF, S)] + [(t, 0, S) for t in range(1, PACK)]
         y_ps = {}
         for t, j0, j1 in parts:
@@ -158,6 +157,8 @@ def tile_picked_cmixhhaarhehh_none_p_kernel(
 
         hz_b = tile("hz_b", [P, S], U8, tag=f"w_w{last}")
         nc.vector.tensor_copy(hz_b[:], xs_tab[:].indirect(hz_l[:]))
+        hz_w = tile("hz_w", [P, S], U32, tag=f"w_b{last}")
+        nc.vector.tensor_copy(hz_w[:], xw_tab[:].indirect(hz_l[:]))
         k2_b = tile("k2_b", [P, H], U8, tag="pa0")
         k1_b = tile("k1_b", [P, H], U8, tag="pa1")
         nc.vector.tensor_copy(k2_b[:], ds_tab[:].indirect(k2_l[:]))

from contextlib import ExitStack

import concourse.mybir as mybir

K, T, S, H, W, G = 512, 1024, 256, 512, 128, 2048
FLOPS = 3 * 2 * K * H * S

F32 = mybir.dt.float32
BF16 = mybir.dt.bfloat16
I32 = mybir.dt.int32
U32 = mybir.dt.uint32
U16 = mybir.dt.uint16
U8 = mybir.dt.uint8
FP8X4 = mybir.dt.float8_e4m3fn_x4
ACT = mybir.ActivationFunctionType
ALU = mybir.AluOpType

P = 128
PACK = 4
HALF = S // 2
SCALAR_M = 22


def tile_picked_cmixhhaarhehh_none_p_kernel(
    tc, x_words, x_scales, w1, gs, d_words, d_scales, sl, th, offs, n1, n2, n3, k1, k2, hz, n4, n5, out
):
    nc = tc.nc
    planes = range(PACK)
    halves = range(2)
    last = PACK - 1

    with ExitStack() as ctx:
        lists = ctx.enter_context(tc.tile_pool(name="lists", bufs=1))
        sb = ctx.enter_context(tc.tile_pool(name="sb", bufs=1))
        psum = ctx.enter_context(tc.psum_pool(name="psum", bufs=1))

        def tile(name, shape, dtype, tag=""):
            return sb.tile(shape, dtype, name=name, tag=tag or name, align_bytes=64)

        def load_list(name, src):
            dst = lists.tile(list(src.shape), U16, name=name)
            nc.sync.dma_start(dst[:], src)
            return dst

        def as_words(packed):
            return packed[0].rearrange("p n r -> p (n r)").bitcast(I32)

        xs_tab = tile("xs_tab", [P, T], U8)
        nc.vector.memset(xs_tab[:].bitcast(I32), 0)

        warm_in = tile("warm_in", [P, 1], F32)
        warm_out = tile("warm_out", [P, 1], F32)
        nc.gpsimd.memset(warm_in[:], 0.0)
        nc.scalar.activation(warm_out[:], warm_in[:], ACT.Sigmoid)

        ds_tab = tile("ds_tab", [P, G], U8)
        nc.vector.memset(ds_tab[:].bitcast(I32), 0)
        placed = tile("placed", [P, H], U8)
        nc.vector.memset(placed[:].bitcast(I32), 0)
        hz_s = tile("hz_s", [P, S], U8)
        nc.vector.memset(hz_s[:].bitcast(I32), 0)

        w_rows = w1.rearrange("(p j) c -> p j c", j=PACK)
        w_raw = [tile(f"w_raw{u}", [P, PACK, H // 2], F32) for u in halves]
        nc.sync.dma_start(w_raw[0][:], w_rows[:, :, 0 : H // 2])
        offs_l = load_list("offs_l", offs)
        xs_rows = x_scales[0].bitcast(I32)
        for b in range(2):
            nc.sync.dma_start(xs_tab[b:P:16, :].bitcast(I32), xs_rows[b:16:2, :])
        for a in (2, 3):
            nc.sync.dma_start(xs_tab[a:P:32, :].bitcast(I32), xs_rows[a:16:4, :])
        nc.sync.dma_start(w_raw[1][:], w_rows[:, :, H // 2 : H])
        xw_tab = tile("xw_tab", [P, T], U32)
        nc.sync.dma_start(xw_tab[:].bitcast(I32), as_words(x_words))
        hz_l = load_list("hz_l", hz)
        ds_rows = d_scales[0].bitcast(I32)
        for b in range(2):
            nc.sync.dma_start(ds_tab[b:P:16, :].bitcast(I32), ds_rows[b:16:2, :])
        k2_l = load_list("k2_l", k2)
        n1_l = load_list("n1_l", n1)
        n2_l = load_list("n2_l", n2)
        n3_l = load_list("n3_l", n3)
        k1_l = load_list("k1_l", k1)
        dw_tab = tile("dw_tab", [P, G], U32)
        nc.sync.dma_start(dw_tab[:].bitcast(I32), as_words(d_words))

        def load_by_row(name, src):
            dst = tile(name, [P, PACK], F32)
            nc.sync.dma_start(dst[:], src.rearrange("(p t) o -> p (t o)", t=PACK))
            return dst

        gs_t = load_by_row("gs_t", gs)
        n4_l = load_list("n4_l", n4)
        n5_l = load_list("n5_l", n5)
        sl_t = load_by_row("sl_t", sl)
        th_t = load_by_row("th_t", th)

        xq_b = tile("xq_b", [P, S], U8)
        xq_w = tile("xq_w", [P, S], U32)
        nc.vector.tensor_copy(xq_b[:], xs_tab[:].indirect(offs_l[:]))

        w_bf = tile("w_bf", [P, PACK, P, PACK], BF16)

        def deal_w(copy, u, m0, m1):
            copy(
                w_bf[:, :, 64 * u + m0 : 64 * u + m1, :].rearrange("p t m j -> p m t j"),
                w_raw[u][:, :, PACK * m0 : PACK * m1].rearrange("p j (m t) -> p m t j", t=PACK),
            )

        deal_w(nc.scalar.copy, 0, 0, 64)
        deal_w(nc.scalar.copy, 1, 0, SCALAR_M)
        deal_w(nc.vector.tensor_copy, 1, SCALAR_M, 64)

        w_w = [tile(f"w_w{t}", [P, P], U32) for t in planes]
        w_b = [tile(f"w_b{t}", [P, P], U8) for t in planes]
        for t in planes:
            nc.vector.quantize_mx(
                out=w_w[t][:].bitcast(FP8X4), scales=w_b[t][:], in_=w_bf[:, t, :, :].rearrange("p m j -> p (m j)")
            )
        for j0 in (0, HALF):
            nc.vector.tensor_copy(xq_w[:, j0 : j0 + HALF], xw_tab[:].indirect(offs_l[:, j0 // 16 : (j0 + HALF) // 16]))
        parts = [(0, 0, HALF), (0, HALF, S)] + [(t, 0, S) for t in range(1, PACK)]
        y_ps = {}
        for t, j0, j1 in parts:
            acc = psum.tile([P, j1 - j0], F32, name=f"y_ps{t}_{j0}", tag=f"bank{t}_{j0}")
            nc.tensor.matmul_mx(
                out=acc[:], lhsT=w_w[t][:].bitcast(FP8X4), lhsT_scale=w_b[t][:],
                rhs=xq_w[:, j0:j1].bitcast(FP8X4), rhs_scale=xq_b[:, j0:j1], start=True, stop=True,
            )
            y_ps[t, j0] = acc

        dt_win = [tile(f"dt_win{t}", [P, 2 * S], F32) for t in planes]
        h_win = [tile(f"h_win{t}", [P, 2 * S], F32) for t in planes]
        st_win = [tile(f"st_win{t}", [P, 2 * S], F32) for t in planes]
        y = [dt_win[t][:, S:] for t in planes]
        far = [h_win[t][:, S:] for t in planes]
        near = [st_win[t][:, S:] for t in planes]
        pa, pb, ra, rb = (
            [tile(f"{name}{u}", [P, 2 * W], F32) for u in halves] for name in ("pa", "pb", "ra", "rb")
        )

        def of(pairs, t):
            return pairs[t // 2][:, t % 2 * W : (t % 2 + 1) * W]

        for t, j0, j1 in parts:
            if t == 0:
                nc.scalar.activation(y[t][:, j0:j1], y_ps[t, j0][:], ACT.Copy)
            else:
                nc.vector.tensor_copy(y[t][:, j0:j1], y_ps[t, j0][:])
        for t in planes:
            nc.scalar.activation(of(pa, t), y[t].indirect(n1_l[:]), ACT.Copy)
            nc.scalar.activation(of(pb, t), y[t].indirect(n2_l[:]), ACT.Copy)
            if t % 2:
                u = t // 2
                nc.vector.tensor_tensor(ra[u][:], pa[u][:], pb[u][:], ALU.add)
                nc.vector.tensor_tensor(rb[u][:], pa[u][:], pb[u][:], ALU.subtract)

        hz_b = tile("hz_b", [P, S], U8, tag=f"w_w{last}")
        nc.vector.tensor_copy(hz_b[:], xs_tab[:].indirect(hz_l[:]))
        hz_w = tile("hz_w", [P, S], U32, tag=f"w_b{last}")
        nc.vector.tensor_copy(hz_w[:], xw_tab[:].indirect(hz_l[:]))
        k2_b = tile("k2_b", [P, H], U8, tag="pa0")
        k1_b = tile("k1_b", [P, H], U8, tag="pa1")
        nc.vector.tensor_copy(k2_b[:], ds_tab[:].indirect(k2_l[:]))
        nc.vector.tensor_copy(k1_b[:], ds_tab[:].indirect(k1_l[:]))
        for dst, first, got in ((hz_s, 0, hz_b), (placed, 4, k2_b), (placed, 0, k1_b)):
            for a in range(4):
                src = 16 * (a // 2) + a % 2
                nc.sync.dma_start(dst[first + a : P : 32, :].bitcast(I32), got[src:P:32, :].bitcast(I32))

        got_w = tile("got_w", [P, 2 * H], U32)
        dealt_w = tile("dealt_w", [P, 2 * H], U32)
        for c, k_l in ((1, k2_l), (0, k1_l)):
            nc.vector.tensor_copy(got_w[:, c * H : (c + 1) * H], dw_tab[:].indirect(k_l[:]))
        for c in (1, 0):
            cols = slice(c * H, (c + 1) * H)
            nc.vector.tensor_copy(
                dealt_w[:, cols].rearrange("p (t g i) -> p g t i", t=PACK, i=4),
                got_w[:, cols].rearrange("p (g i t) -> p g t i", t=PACK, i=4),
            )
        dealt_b = tile("dealt_b", [P, H], U8)
        nc.vector.tensor_copy(
            dealt_b[:].rearrange("p (t g i) -> p g t i", t=PACK, i=16),
            placed[:].rearrange("p (g i t) -> p g t i", t=PACK, i=16),
        )

        nbias = tile("nbias", [P, PACK], F32, tag="pb1")
        nc.vector.scalar_tensor_tensor(nbias[:], sl_t[:], -1.0, th_t[:], ALU.mult, ALU.mult)

        h_ps = {}
        for t, j0, j1 in parts:
            acc = psum.tile([P, j1 - j0], F32, name=f"h_ps{t}_{j0}", tag=f"bank{t}_{j0}")
            cols = slice(H + t * P, H + (t + 1) * P)
            nc.tensor.matmul_mx(
                out=acc[:], lhsT=dealt_w[:, cols].bitcast(FP8X4), lhsT_scale=dealt_b[4:P, t * P : (t + 1) * P],
                rhs=hz_w[:, j0:j1].bitcast(FP8X4), rhs_scale=hz_s[:, j0:j1],
                start=True, stop=False,
            )
            h_ps[t, j0] = acc

        z_bf = tile("z_bf", [P, S, PACK], BF16, tag="got_w")
        top = tile("top", [P, PACK * S], F32, tag="placed")

        def put_sum(t):
            nc.scalar.activation(dt_win[t][:].indirect(n1_l[:]), of(ra, t), ACT.Copy)

        def put_difference(t):
            nc.scalar.activation(dt_win[t][:].indirect(n2_l[:]), of(rb, t), ACT.Copy)

        def make_z(t, j0, j1):
            nc.scalar.activation(far[t][:, j0:j1], dt_win[t][:].indirect(n3_l[:, j0 // 16 : j1 // 16]), ACT.Copy)
            larger = top[:, t * S + j0 : t * S + j1]
            nc.vector.tensor_tensor(larger, dt_win[t][:, j0:j1], far[t][:, j0:j1], ALU.max)
            nc.vector.tensor_scalar(z_bf[:, j0:j1, t], larger, gs_t[:, t : t + 1], None, ALU.mult)

        z_w = tile("z_w", [P, S], U32)
        z_b = tile("z_b", [P, S], U8)

        def quantise_z(j0, j1):
            nc.vector.quantize_mx(
                out=z_w[:, j0:j1].bitcast(FP8X4), scales=z_b[:, j0:j1],
                in_=z_bf[:, j0:j1, :].rearrange("p j t -> p (j t)"),
            )

        put_sum(0)
        put_sum(1)
        put_difference(0)
        put_sum(2)
        put_difference(1)
        make_z(0, 0, S)
        put_difference(2)
        make_z(1, 0, S)
        put_sum(3)
        make_z(2, 0, HALF)
        put_difference(3)
        make_z(2, HALF, S)
        make_z(3, 0, HALF)
        quantise_z(0, HALF)
        make_z(3, HALF, S - 64)
        quantise_z(HALF, S - 64)
        make_z(3, S - 64, S)
        quantise_z(S - 64, S)

        for t, j0, j1 in parts:
            cols = slice(t * P, (t + 1) * P)
            acc = h_ps[t, j0]
            nc.tensor.matmul_mx(
                out=acc[:], lhsT=dealt_w[:, cols].bitcast(FP8X4), lhsT_scale=dealt_b[:, cols],
                rhs=z_w[:, j0:j1].bitcast(FP8X4), rhs_scale=z_b[:, j0:j1], start=False, stop=True,
            )
            if t == 0:
                nc.scalar.activation(h_win[t][:, j0:j1], acc[:], ACT.Copy, scale=0.0625)
            else:
                nc.vector.tensor_scalar(h_win[t][:, j0:j1], acc[:], 0.0625, None, ALU.mult)

        out_rows = out.rearrange("(p t) j -> p t j", t=PACK)

        def neighbour(t):
            nc.scalar.activation(near[t], h_win[t][:].indirect(n4_l[:]), ACT.Copy)
            nc.vector.tensor_tensor(st_win[t][:, 0:S], h_win[t][:, 0:S], near[t], ALU.max)

        def gate(t, j0, j1):
            sg = tile(f"sg{t}_{j0}", [P, j1 - j0], F32)
            nc.scalar.activation(
                sg[:], st_win[t][:].indirect(n5_l[:, j0 // 16 : j1 // 16]), ACT.Sigmoid,
                bias=nbias[:, t : t + 1], scale=sl_t[:, t : t + 1],
            )
            res = tile(f"res{t}_{j0}", [P, j1 - j0], F32)
            nc.vector.tensor_tensor(res[:], st_win[t][:, j0:j1], sg[:], ALU.mult)
            nc.sync.dma_start(out_rows[:, t, j0:j1], res[:])

        neighbour(0)
        for t in range(last):
            neighbour(t + 1)
            gate(t, 0, S)
        gate(last, 0, HALF)
        gate(last, HALF, S)
